import numpy as np, ml_dtypes
CORES = [32,160,288,416,80,208,336,464]
N = 8
KB, QP, ROOT = 2, 32, 7
def setup_inputs(rng):
    return {"q": rng.standard_normal((N, 128, QP), dtype=np.float32).astype(ml_dtypes.bfloat16), "k": rng.standard_normal((N, 128, KB * 128), dtype=np.float32).astype(ml_dtypes.bfloat16), "v": rng.standard_normal((N, 128, KB * 128), dtype=np.float32).astype(ml_dtypes.bfloat16)}
def setup_inputs_big(rng):
    d = setup_inputs(rng)
    for k in ("q", "k", "v"): d[k] = (d[k].astype(np.float32) * 1024.0).astype(d[k].dtype)
    return d
def setup_inputs_small(rng):
    d = setup_inputs(rng)
    for k in ("q", "k", "v"): d[k] = (d[k].astype(np.float32) * (1 / 1024.0)).astype(d[k].dtype)
    return d
def setup_inputs_apart(rng):
    d = setup_inputs(rng)
    f = (10.0 ** rng.permutation(np.linspace(-1.5, 1.5, N))).astype(np.float32).reshape(N, 1, 1)
    for k in ("q", "k", "v"): d[k] = (d[k].astype(np.float32) * f).astype(d[k].dtype)
    return d
def reference(q, k, v):
    Q, K, V = q.astype(np.float64), k.astype(np.float64), v.astype(np.float64)
    o = np.zeros((128, QP))
    for j in range(N):
        for b in range(KB):
            o += V[j][:, 128 * b:128 * b + 128].T @ np.maximum(K[j][:, 128 * b:128 * b + 128].T @ Q[ROOT], 0.0)
    y = np.full((N, 128, QP), np.nan)
    y[ROOT] = o
    return {"y": y.astype(ml_dtypes.bfloat16 if q.dtype != np.float64 else np.float64)}

@@ -1,0 +1,169 @@
+from concourse.bass import DstId, RemoteDMATransfer
+from concourse.mybir import AluOpType
+
+QP = 32
+BW = 128
+KB = 2
+KW = KB * BW
+W = 2 * KW
+SW = KB * QP
+GMAX = 3
+NSITE = 5
+
+NEAR_SITES = 1
+NQ = 8
+NSHIP = 8
+NO = 8
+
+SCRATCH = {
+    "qs": ("sbuf", [128, QP], "bfloat16"),
+    "kv": ("sbuf", [128, W], "bfloat16"),
+    "gkv": ("sbuf", [128, GMAX * W], "bfloat16"),
+    "zero": ("sbuf", [128, SW], "float32"),
+    "sb": ("sbuf", [128, (GMAX + 1) * SW], "bfloat16"),
+    "ob": ("sbuf", [128, QP], "bfloat16"),
+    "land": ("sbuf", [128, NSITE * QP], "bfloat16"),
+    "acc": ("sbuf", [128, NSITE * QP], "float32"),
+    "ps0": ("psum", [128, 512], "float32"),
+    "ps1": ("psum", [128, 512], "float32"),
+    "ps2": ("psum", [128, 512], "float32"),
+    "ps3": ("psum", [128, 512], "float32"),
+    "po": ("psum", [128, 512], "float32"),
+}
+SEMAPHORES = (["sq", "sl", "sz", "so", "sc", "sv", "sx", "sy"]
+              + ["sg%d" % i for i in range(GMAX)]
+              + ["sm%d" % i for i in range(GMAX + 1)]
+              + ["sr%d" % i for i in range(GMAX + 1)]
+              + ["sa%d" % i for i in range(NSITE)])
+
+
+def _plan(T, topo):
+    cores = list(T.cores)
+    n = len(cores)
+    root = T.root
+    rc = cores[root]
+    site = [None] * n
+    site[root] = root
+    near, far = [], []
+    for r in range(n):
+        if r == root:
+            continue
+        c = cores[r]
+        if not (topo.may_write(rc, c) and topo.may_write(c, rc)):
+            far.append(r)
+        elif topo.same_plane(c, rc):
+            near.append(r)
+        else:
+            site[r] = r
+    for i, r in enumerate(near):
+        site[r] = r if i < NEAR_SITES else root
+    load = dict((s, 0) for s in range(n) if site[s] == s and s != root)
+    for r in far:
+        c = cores[r]
+        cand = [s for s in load if topo.may_write(c, cores[s])]
+        s = min(cand, key=lambda s: (not topo.same_plane(c, cores[s]), load[s],
+                                     topo.chip(cores[s]) != topo.chip(c), s))
+        site[r] = s
+        load[s] += 1
+    guests = dict((s, [r for r in range(n) if site[r] == s and r != s]) for s in range(n) if site[s] == s)
+    sites = sorted((s for s in guests if s != root), key=lambda s: (len(guests[s]), s))
+    return site, guests, sites
+
+
+def _engines(mask, n):
+    bits = [i for i in range(16) if (mask >> i) & 1]
+    m = 0
+    for i in bits[::len(bits) // n][:n]:
+        m |= 1 << i
+    return m
+
+
+def rank_program(g, core, T, topo):
+    rank = T.rank_of(core)
+    if rank is None:
+        return
+    S = T.sem
+    root = T.root
+    cores = list(T.cores)
+    site, guests, sites = _plan(T, topo)
+    is_root = rank == root
+
+    if is_root:
+        g.sync.dma_start(T.qs[:], T.q[:]).then_inc(S.sq, 16)
+        g.sync.wait_ge(S.sq, 16)
+        g.scalar.wait_ge(S.sq, 16)
+    g.sync.dma_start(T.kv[:, 0:KW], T.k[:]).then_inc(S.sl, 16)
+    g.scalar.dma_start(T.kv[:, KW:W], T.v[:]).then_inc(S.sl, 16)
+
+    if site[rank] != rank:
+        d = cores[site[rank]]
+        slot = guests[site[rank]].index(rank)
+        rid, pid = topo.addr(d, core)
+        g.wait_ge(S.sl, 32)
+        g.remote_dma(out_ap=T.gkv[:, slot * W:(slot + 1) * W], in_ap=T.kv[:], remote_sem=S["sg%d" % slot],
+                     local_sem=S.sx, pid=pid, routing_id=rid, dma_engine_mask=_engines(topo.mask(core, d), NSHIP))
+        g.wait_ge(S.sx, NSHIP)
+        return
+
+    if is_root:
+        m = topo.mask(core, cores[sites[0]])
+        ids = []
+        for s in sites:
+            m &= topo.mask(core, cores[s])
+            rid, pid = topo.addr(cores[s], core)
+            ids.append(DstId(rid=rid, pnc=pid))
+        g.wait_ge(S.sq, 16)
+        g.remote_dma_fused([RemoteDMATransfer(dst_ids=ids, dma_engine_mask=_engines(m, NQ), remote_sem=S.sq,
+                                              srcs=[T.qs[:]], dsts=[T.qs[:] for s in sites], alu_op=0)],
+                           local_sem=S.sx)
+
+    g.vector.memset(T.zero[:], 0.0).then_inc(S.sz, 1)
+    g.vector.wait_ge(S.sz, 1)
+    ngroups = 1 + len(guests[rank])
+    g.tensor.wait_ge(S.sq, 16 if is_root else NQ)
+    for i in range(ngroups):
+        if i == 0:
+            buf, base = T.kv, 0
+            g.tensor.wait_ge(S.sl, 32)
+        else:
+            buf, base = T.gkv, (i - 1) * W
+            g.tensor.wait_ge(S["sg%d" % (i - 1)], NSHIP)
+        ps = T["ps%d" % i]
+        for b in range(KB):
+            g.tensor.matmul(ps[:, b * QP:(b + 1) * QP], buf[:, base + b * BW:base + (b + 1) * BW], T.qs[:],
+                            start=True, stop=True).then_inc(S["sm%d" % i], 1)
+        g.vector.wait_ge(S["sm%d" % i], KB)
+        g.vector.tensor_tensor(T.sb[:, i * SW:(i + 1) * SW], ps[:, 0:SW], T.zero[:],
+                               AluOpType.max).then_inc(S["sr%d" % i], 1)
+        g.tensor.wait_ge(S["sr%d" % i], 1)
+        for b in range(KB):
+            g.tensor.matmul(T.po[:, 0:QP], buf[:, base + KW + b * BW:base + KW + (b + 1) * BW],
+                            T.sb[:, i * SW + b * QP:i * SW + (b + 1) * QP],
+                            start=(i == 0 and b == 0), stop=(i == ngroups - 1 and b == KB - 1)).then_inc(S.so, 1)
+    g.vector.wait_ge(S.so, KB * ngroups)
+
+    if not is_root:
+        j = sites.index(rank)
+        d = cores[root]
+        rid, pid = topo.addr(d, core)
+        g.vector.tensor_copy(T.ob[:], T.po[:, 0:QP]).then_inc(S.sc, 1)
+        g.wait_ge(S.sc, 1)
+        g.remote_dma(out_ap=T.land[:, j * QP:(j + 1) * QP], in_ap=T.ob[:], remote_sem=S["sa%d" % j],
+                     local_sem=S.sx, pid=pid, routing_id=rid, dma_engine_mask=_engines(topo.mask(core, d), NO))
+        g.wait_ge(S.sx, NO)
+        return
+
+    prev = T.po[:, 0:QP]
+    for j in range(len(sites)):
+        last = j == len(sites) - 1
+        g.vector.wait_ge(S["sa%d" % j], NO)
+        if j > 0:
+            g.vector.wait_ge(S.sv, j)
+        out = T.ob[:] if last else T.acc[:, j * QP:(j + 1) * QP]
+        g.vector.tensor_tensor(out, prev, T.land[:, j * QP:(j + 1) * QP],
+                               AluOpType.add).then_inc(S.sc if last else S.sv, 1)
+        prev = out
+    g.sync.wait_ge(S.sc, 1)
+    g.sync.dma_start(T.y[:], T.ob[:]).then_inc(S.sy, 16)
+    g.sync.wait_ge(S.sy, 16)
+    g.wait_ge(S.sx, NQ)

@@ -16,6 +16,9 @@ NSHIP = 8
 NO = 8
 
 SCRATCH = {
+    "qd": ("dram", [128, QP], "bfloat16"),
+    "kd": ("dram", [128, KW], "bfloat16"),
+    "vd": ("dram", [128, KW], "bfloat16"),
     "qs": ("sbuf", [128, QP], "bfloat16"),
     "kv": ("sbuf", [128, W], "bfloat16"),
     "gkv": ("sbuf", [128, GMAX * W], "bfloat16"),
@@ -30,8 +33,9 @@ SCRATCH = {
     "ps3": ("psum", [128, 512], "float32"),
     "po": ("psum", [128, 512], "float32"),
 }
-SEMAPHORES = (["sq", "sl", "sz", "so", "sc", "sv", "sx", "sy"]
-              + ["sg%d" % i for i in range(GMAX)]
+SEMAPHORES = (["sqd", "sq", "slk", "slv", "sz", "so", "sc", "sv", "sx", "sy"]
+              + ["sgk%d" % i for i in range(GMAX)]
+              + ["sgv%d" % i for i in range(GMAX)]
               + ["sm%d" % i for i in range(GMAX + 1)]
               + ["sr%d" % i for i in range(GMAX + 1)]
               + ["sa%d" % i for i in range(NSITE)])
@@ -88,22 +92,29 @@ def rank_program(g, core, T, topo):
     site, guests, sites = _plan(T, topo)
     is_root = rank == root
 
-    if is_root:
-        g.sync.dma_start(T.qs[:], T.q[:]).then_inc(S.sq, 16)
-        g.sync.wait_ge(S.sq, 16)
-        g.scalar.wait_ge(S.sq, 16)
-    g.sync.dma_start(T.kv[:, 0:KW], T.k[:]).then_inc(S.sl, 16)
-    g.scalar.dma_start(T.kv[:, KW:W], T.v[:]).then_inc(S.sl, 16)
-
     if site[rank] != rank:
         d = cores[site[rank]]
         slot = guests[site[rank]].index(rank)
         rid, pid = topo.addr(d, core)
-        g.wait_ge(S.sl, 32)
-        g.remote_dma(out_ap=T.gkv[:, slot * W:(slot + 1) * W], in_ap=T.kv[:], remote_sem=S["sg%d" % slot],
-                     local_sem=S.sx, pid=pid, routing_id=rid, dma_engine_mask=_engines(topo.mask(core, d), NSHIP))
-        g.wait_ge(S.sx, NSHIP)
+        m = _engines(topo.mask(core, d), NSHIP)
+        g.sync.dma_start(T.kd[:], T.k[:]).then_inc(S.slk, 16)
+        g.scalar.dma_start(T.vd[:], T.v[:]).then_inc(S.slv, 16)
+        g.wait_ge(S.slk, 16)
+        g.remote_dma(out_ap=T.gkv[:, slot * W:slot * W + KW], in_ap=T.kd[:], remote_sem=S["sgk%d" % slot],
+                     local_sem=S.sx, pid=pid, routing_id=rid, dma_engine_mask=m)
+        g.wait_ge(S.slv, 16)
+        g.remote_dma(out_ap=T.gkv[:, slot * W + KW:(slot + 1) * W], in_ap=T.vd[:], remote_sem=S["sgv%d" % slot],
+                     local_sem=S.sx, pid=pid, routing_id=rid, dma_engine_mask=m)
+        g.wait_ge(S.sx, 2 * NSHIP)
         return
+
+    if is_root:
+        g.sync.dma_start(T.qd[:], T.q[:]).then_inc(S.sqd, 16)
+        g.sync.wait_ge(S.sqd, 16)
+        g.scalar.wait_ge(S.sqd, 16)
+        g.scalar.dma_start(T.qs[:], T.q[:]).then_inc(S.sq, 16)
+    g.sync.dma_start(T.kv[:, 0:KW], T.k[:]).then_inc(S.slk, 16)
+    g.scalar.dma_start(T.kv[:, KW:W], T.v[:]).then_inc(S.slv, 16)
 
     if is_root:
         m = topo.mask(core, cores[sites[0]])
@@ -112,22 +123,24 @@ def rank_program(g, core, T, topo):
             m &= topo.mask(core, cores[s])
             rid, pid = topo.addr(cores[s], core)
             ids.append(DstId(rid=rid, pnc=pid))
-        g.wait_ge(S.sq, 16)
+        g.wait_ge(S.sqd, 16)
         g.remote_dma_fused([RemoteDMATransfer(dst_ids=ids, dma_engine_mask=_engines(m, NQ), remote_sem=S.sq,
-                                              srcs=[T.qs[:]], dsts=[T.qs[:] for s in sites], alu_op=0)],
+                                              srcs=[T.qd[:]], dsts=[T.qs[:] for s in sites], alu_op=0)],
                            local_sem=S.sx)
 
     g.vector.memset(T.zero[:], 0.0).then_inc(S.sz, 1)
     g.vector.wait_ge(S.sz, 1)
     ngroups = 1 + len(guests[rank])
-    g.tensor.wait_ge(S.sq, 16 if is_root else NQ)
-    for i in range(ngroups):
+
+    def where(i):
+        return (T.kv, 0) if i == 0 else (T.gkv, (i - 1) * W)
+
+    def scores(i):
+        buf, base = where(i)
         if i == 0:
-            buf, base = T.kv, 0
-            g.tensor.wait_ge(S.sl, 32)
+            g.tensor.wait_ge(S.slk, 16)
         else:
-            buf, base = T.gkv, (i - 1) * W
-            g.tensor.wait_ge(S["sg%d" % (i - 1)], NSHIP)
+            g.tensor.wait_ge(S["sgk%d" % (i - 1)], NSHIP)
         ps = T["ps%d" % i]
         for b in range(KB):
             g.tensor.matmul(ps[:, b * QP:(b + 1) * QP], buf[:, base + b * BW:base + (b + 1) * BW], T.qs[:],
@@ -135,11 +148,25 @@ def rank_program(g, core, T, topo):
         g.vector.wait_ge(S["sm%d" % i], KB)
         g.vector.tensor_tensor(T.sb[:, i * SW:(i + 1) * SW], ps[:, 0:SW], T.zero[:],
                                AluOpType.max).then_inc(S["sr%d" % i], 1)
+
+    def values(i):
+        buf, base = where(i)
+        if i == 0:
+            g.tensor.wait_ge(S.slv, 16)
+        else:
+            g.tensor.wait_ge(S["sgv%d" % (i - 1)], NSHIP)
         g.tensor.wait_ge(S["sr%d" % i], 1)
         for b in range(KB):
             g.tensor.matmul(T.po[:, 0:QP], buf[:, base + KW + b * BW:base + KW + (b + 1) * BW],
                             T.sb[:, i * SW + b * QP:i * SW + (b + 1) * QP],
                             start=(i == 0 and b == 0), stop=(i == ngroups - 1 and b == KB - 1)).then_inc(S.so, 1)
+
+    g.tensor.wait_ge(S.sq, 16 if is_root else NQ)
+    for i in range(ngroups):
+        scores(i)
+        if i > 0:
+            values(i - 1)
+    values(ngroups - 1)
     g.vector.wait_ge(S.so, KB * ngroups)
 
     if not is_root:

@@ -7,37 +7,44 @@ KB = 2
 KW = KB * BW
 W = 2 * KW
 SW = KB * QP
-GMAX = 3
-NSITE = 5
+GMAX = 2
+NSITE = 3
+NGRP = 2 + GMAX
+HP = 32
 
 NEAR_SITES = 1
+NEAR_GUESTS = 1
 NQ = 8
 NSHIP = 8
 NO = 8
+NH = 8
 
 SCRATCH = {
     "qd": ("dram", [128, QP], "bfloat16"),
     "kd": ("dram", [128, KW], "bfloat16"),
     "vd": ("dram", [128, KW], "bfloat16"),
+    "hd": ("dram", [128, 2 * HP], "bfloat16"),
+    "hl": ("dram", [NSITE, 128, 2 * HP], "bfloat16"),
     "qs": ("sbuf", [128, QP], "bfloat16"),
     "kv": ("sbuf", [128, W], "bfloat16"),
     "gkv": ("sbuf", [128, GMAX * W], "bfloat16"),
+    "hk": ("sbuf", [128, NSITE * HP], "bfloat16"),
+    "hv": ("sbuf", [128, BW], "bfloat16"),
     "zero": ("sbuf", [128, SW], "float32"),
-    "sb": ("sbuf", [128, (GMAX + 1) * SW], "bfloat16"),
+    "sb": ("sbuf", [128, NGRP * SW], "bfloat16"),
     "ob": ("sbuf", [128, QP], "bfloat16"),
     "land": ("sbuf", [128, NSITE * QP], "bfloat16"),
     "acc": ("sbuf", [128, NSITE * QP], "float32"),
-    "ps0": ("psum", [128, 512], "float32"),
-    "ps1": ("psum", [128, 512], "float32"),
-    "ps2": ("psum", [128, 512], "float32"),
-    "ps3": ("psum", [128, 512], "float32"),
     "po": ("psum", [128, 512], "float32"),
 }
-SEMAPHORES = (["sqd", "sq", "slk", "slv", "sz", "so", "sc", "sv", "sx", "sy"]
+for _i in range(NGRP):
+    SCRATCH["ps%d" % _i] = ("psum", [128, 512], "float32")
+SEMAPHORES = (["sqd", "sq", "slk", "slv", "slh", "shk", "shv", "sz", "so", "sc", "sv", "sx", "sy"]
               + ["sgk%d" % i for i in range(GMAX)]
               + ["sgv%d" % i for i in range(GMAX)]
-              + ["sm%d" % i for i in range(GMAX + 1)]
-              + ["sr%d" % i for i in range(GMAX + 1)]
+              + ["sh%d" % i for i in range(NSITE)]
+              + ["sm%d" % i for i in range(NGRP)]
+              + ["sr%d" % i for i in range(NGRP)]
               + ["sa%d" % i for i in range(NSITE)])
 
 
@@ -60,8 +67,13 @@ def _plan(T, topo):
         else:
             site[r] = r
     for i, r in enumerate(near):
-        site[r] = r if i < NEAR_SITES else root
-    load = dict((s, 0) for s in range(n) if site[s] == s and s != root)
+        if i < NEAR_SITES:
+            site[r] = r
+        elif i < NEAR_SITES + NEAR_GUESTS:
+            site[r] = near[(i - NEAR_SITES) % NEAR_SITES]
+        else:
+            site[r] = root
+    load = dict((s, 0) for s in range(n) if site[s] == s and s != root and s not in near)
     for r in far:
         c = cores[r]
         cand = [s for s in load if topo.may_write(c, cores[s])]
@@ -70,7 +82,8 @@ def _plan(T, topo):
         site[r] = s
         load[s] += 1
     guests = dict((s, [r for r in range(n) if site[r] == s and r != s]) for s in range(n) if site[s] == s)
-    sites = sorted((s for s in guests if s != root), key=lambda s: (len(guests[s]), s))
+    sites = sorted((s for s in guests if s != root),
+                   key=lambda s: (not topo.same_plane(rc, cores[s]), topo.chip(cores[s]) != topo.chip(rc), s))
     return site, guests, sites
 
 
@@ -91,6 +104,8 @@ def rank_program(g, core, T, topo):
     cores = list(T.cores)
     site, guests, sites = _plan(T, topo)
     is_root = rank == root
+    hb = (KB - 1) * BW
+    keep = BW - HP
 
     if site[rank] != rank:
         d = cores[site[rank]]
@@ -113,13 +128,16 @@ def rank_program(g, core, T, topo):
         g.sync.wait_ge(S.sqd, 16)
         g.scalar.wait_ge(S.sqd, 16)
         g.scalar.dma_start(T.qs[:], T.q[:]).then_inc(S.sq, 16)
+    else:
+        g.sync.dma_start(T.hd[0:64, :], T.k[:, hb + keep:hb + BW]).then_inc(S.slh, 16)
+        g.scalar.dma_start(T.hd[64:128, :], T.v[keep:BW, hb:hb + BW]).then_inc(S.slh, 16)
     g.sync.dma_start(T.kv[:, 0:KW], T.k[:]).then_inc(S.slk, 16)
     g.scalar.dma_start(T.kv[:, KW:W], T.v[:]).then_inc(S.slv, 16)
 
     if is_root:
         m = topo.mask(core, cores[sites[0]])
         ids = []
-        for s in sites:
+        for s in sites[::-1]:
             m &= topo.mask(core, cores[s])
             rid, pid = topo.addr(cores[s], core)
             ids.append(DstId(rid=rid, pnc=pid))
@@ -127,39 +145,57 @@ def rank_program(g, core, T, topo):
         g.remote_dma_fused([RemoteDMATransfer(dst_ids=ids, dma_engine_mask=_engines(m, NQ), remote_sem=S.sq,
                                               srcs=[T.qd[:]], dsts=[T.qs[:] for s in sites], alu_op=0)],
                            local_sem=S.sx)
+        for i in range(len(sites)):
+            g.sync.wait_ge(S["sh%d" % i], NH)
+            g.sync.dma_start(T.hk[:, i * HP:(i + 1) * HP], T.hl[i, 0:64, :]).then_inc(S.shk, 16)
+            g.scalar.wait_ge(S["sh%d" % i], NH)
+            g.scalar.dma_start(T.hv[i * HP:(i + 1) * HP, :], T.hl[i, 64:128, :]).then_inc(S.shv, 16)
+    else:
+        j = sites.index(rank)
+        d = cores[root]
+        rrid, rpid = topo.addr(d, core)
+        rmask = topo.mask(core, d)
+        g.wait_ge(S.slh, 32)
+        g.remote_dma(out_ap=T.hl[j], in_ap=T.hd[:], remote_sem=S["sh%d" % j],
+                     local_sem=S.sx, pid=rpid, routing_id=rrid, dma_engine_mask=_engines(rmask, NH))
+
+    own_k, own_v = [(S.slk, 16)], [(S.slv, 16)]
+    if is_root:
+        groups = [(T.kv, 0, T.kv, KW, KB, BW, own_k, own_v)]
+    else:
+        groups = [(T.kv, 0, T.kv, KW, KB - 1, BW, own_k, own_v), (T.kv, hb, T.kv, KW + hb, 1, keep, [], [])]
+    for i in range(len(guests[rank])):
+        groups.append((T.gkv, i * W, T.gkv, i * W + KW, KB, BW,
+                       [(S["sgk%d" % i], NSHIP)], [(S["sgv%d" % i], NSHIP)]))
+    if is_root:
+        groups.append((T.hk, 0, T.hv, 0, 1, HP * len(sites), [(S.shk, 16 * len(sites))], [(S.shv, 16 * len(sites))]))
+    ngroups = len(groups)
+    nblocks = sum(gr[4] for gr in groups)
 
     g.vector.memset(T.zero[:], 0.0).then_inc(S.sz, 1)
     g.vector.wait_ge(S.sz, 1)
-    ngroups = 1 + len(guests[rank])
-
-    def where(i):
-        return (T.kv, 0) if i == 0 else (T.gkv, (i - 1) * W)
 
     def scores(i):
-        buf, base = where(i)
-        if i == 0:
-            g.tensor.wait_ge(S.slk, 16)
-        else:
-            g.tensor.wait_ge(S["sgk%d" % (i - 1)], NSHIP)
+        kbuf, kc, vbuf, vc, nb, npos, kw, vw = groups[i]
+        for sem, val in kw:
+            g.tensor.wait_ge(sem, val)
         ps = T["ps%d" % i]
-        for b in range(KB):
-            g.tensor.matmul(ps[:, b * QP:(b + 1) * QP], buf[:, base + b * BW:base + (b + 1) * BW], T.qs[:],
+        for b in range(nb):
+            g.tensor.matmul(ps[0:npos, b * QP:(b + 1) * QP], kbuf[:, kc + b * BW:kc + b * BW + npos], T.qs[:],
                             start=True, stop=True).then_inc(S["sm%d" % i], 1)
-        g.vector.wait_ge(S["sm%d" % i], KB)
-        g.vector.tensor_tensor(T.sb[:, i * SW:(i + 1) * SW], ps[:, 0:SW], T.zero[:],
-                               AluOpType.max).then_inc(S["sr%d" % i], 1)
+        g.vector.wait_ge(S["sm%d" % i], nb)
+        g.vector.tensor_tensor(T.sb[0:npos, i * SW:i * SW + nb * QP], ps[0:npos, 0:nb * QP],
+                               T.zero[0:npos, 0:nb * QP], AluOpType.max).then_inc(S["sr%d" % i], 1)
 
     def values(i):
-        buf, base = where(i)
-        if i == 0:
-            g.tensor.wait_ge(S.slv, 16)
-        else:
-            g.tensor.wait_ge(S["sgv%d" % (i - 1)], NSHIP)
+        kbuf, kc, vbuf, vc, nb, npos, kw, vw = groups[i]
+        for sem, val in vw:
+            g.tensor.wait_ge(sem, val)
         g.tensor.wait_ge(S["sr%d" % i], 1)
-        for b in range(KB):
-            g.tensor.matmul(T.po[:, 0:QP], buf[:, base + KW + b * BW:base + KW + (b + 1) * BW],
-                            T.sb[:, i * SW + b * QP:i * SW + (b + 1) * QP],
-                            start=(i == 0 and b == 0), stop=(i == ngroups - 1 and b == KB - 1)).then_inc(S.so, 1)
+        for b in range(nb):
+            g.tensor.matmul(T.po[:, 0:QP], vbuf[0:npos, vc + b * BW:vc + (b + 1) * BW],
+                            T.sb[0:npos, i * SW + b * QP:i * SW + (b + 1) * QP],
+                            start=(i == 0 and b == 0), stop=(i == ngroups - 1 and b == nb - 1)).then_inc(S.so, 1)
 
     g.tensor.wait_ge(S.sq, 16 if is_root else NQ)
     for i in range(ngroups):
@@ -167,17 +203,14 @@ def rank_program(g, core, T, topo):
         if i > 0:
             values(i - 1)
     values(ngroups - 1)
-    g.vector.wait_ge(S.so, KB * ngroups)
+    g.vector.wait_ge(S.so, nblocks)
 
     if not is_root:
-        j = sites.index(rank)
-        d = cores[root]
-        rid, pid = topo.addr(d, core)
         g.vector.tensor_copy(T.ob[:], T.po[:, 0:QP]).then_inc(S.sc, 1)
         g.wait_ge(S.sc, 1)
         g.remote_dma(out_ap=T.land[:, j * QP:(j + 1) * QP], in_ap=T.ob[:], remote_sem=S["sa%d" % j],
-                     local_sem=S.sx, pid=pid, routing_id=rid, dma_engine_mask=_engines(topo.mask(core, d), NO))
-        g.wait_ge(S.sx, NO)
+                     local_sem=S.sx, pid=rpid, routing_id=rrid, dma_engine_mask=_engines(rmask, NO))
+        g.wait_ge(S.sx, NH + NO)
         return
 
     prev = T.po[:, 0:QP]

from concourse.bass import DstId, RemoteDMATransfer
from concourse.mybir import AluOpType

QP = 32
BW = 128
KB = 2
KW = KB * BW
W = 2 * KW
SW = KB * QP
GMAX = 2
NSITE = 3
NGRP = 2 + GMAX
HP = 32

NEAR_SITES = 1
NEAR_GUESTS = 1
NQ = 8
NSHIP = 8
NO = 8
NH = 8

SCRATCH = {
    "qd": ("dram", [128, QP], "bfloat16"),
    "kd": ("dram", [128, KW], "bfloat16"),
    "vd": ("dram", [128, KW], "bfloat16"),
    "hd": ("dram", [128, 2 * HP], "bfloat16"),
    "hl": ("dram", [NSITE, 128, 2 * HP], "bfloat16"),
    "qs": ("sbuf", [128, QP], "bfloat16"),
    "kv": ("sbuf", [128, W], "bfloat16"),
    "gkv": ("sbuf", [128, GMAX * W], "bfloat16"),
    "hk": ("sbuf", [128, NSITE * HP], "bfloat16"),
    "hv": ("sbuf", [128, BW], "bfloat16"),
    "zero": ("sbuf", [128, SW], "float32"),
    "sb": ("sbuf", [128, NGRP * SW], "bfloat16"),
    "ob": ("sbuf", [128, QP], "bfloat16"),
    "land": ("sbuf", [128, NSITE * QP], "bfloat16"),
    "acc": ("sbuf", [128, NSITE * QP], "float32"),
    "po": ("psum", [128, 512], "float32"),
}
for _i in range(NGRP):
    SCRATCH["ps%d" % _i] = ("psum", [128, 512], "float32")
SEMAPHORES = (["sqd", "sq", "slk", "slv", "slh", "shk", "shv", "sz", "so", "sc", "sv", "sx", "sy"]
              + ["sgk%d" % i for i in range(GMAX)]
              + ["sgv%d" % i for i in range(GMAX)]
              + ["sh%d" % i for i in range(NSITE)]
              + ["sm%d" % i for i in range(NGRP)]
              + ["sr%d" % i for i in range(NGRP)]
              + ["sa%d" % i for i in range(NSITE)])


def _plan(T, topo):
    cores = list(T.cores)
    n = len(cores)
    root = T.root
    rc = cores[root]
    site = [None] * n
    site[root] = root
    near, far = [], []
    for r in range(n):
        if r == root:
            continue
        c = cores[r]
        if not (topo.may_write(rc, c) and topo.may_write(c, rc)):
            far.append(r)
        elif topo.same_plane(c, rc):
            near.append(r)
        else:
            site[r] = r
    for i, r in enumerate(near):
        if i < NEAR_SITES:
            site[r] = r
        elif i < NEAR_SITES + NEAR_GUESTS:
            site[r] = near[(i - NEAR_SITES) % NEAR_SITES]
        else:
            site[r] = root
    load = dict((s, 0) for s in range(n) if site[s] == s and s != root and s not in near)
    for r in far:
        c = cores[r]
        cand = [s for s in load if topo.may_write(c, cores[s])]
        s = min(cand, key=lambda s: (not topo.same_plane(c, cores[s]), load[s],
                                     topo.chip(cores[s]) != topo.chip(c), s))
        site[r] = s
        load[s] += 1
    guests = dict((s, [r for r in range(n) if site[r] == s and r != s]) for s in range(n) if site[s] == s)
    sites = sorted((s for s in guests if s != root),
                   key=lambda s: (not topo.same_plane(rc, cores[s]), topo.chip(cores[s]) != topo.chip(rc), s))
    return site, guests, sites


def _engines(mask, n):
    bits = [i for i in range(16) if (mask >> i) & 1]
    m = 0
    for i in bits[::len(bits) // n][:n]:
        m |= 1 << i
    return m


def rank_program(g, core, T, topo):
    rank = T.rank_of(core)
    if rank is None:
        return
    S = T.sem
    root = T.root
    cores = list(T.cores)
    site, guests, sites = _plan(T, topo)
    is_root = rank == root
    hb = (KB - 1) * BW
    keep = BW - HP

    if site[rank] != rank:
        d = cores[site[rank]]
        slot = guests[site[rank]].index(rank)
        rid, pid = topo.addr(d, core)
        m = _engines(topo.mask(core, d), NSHIP)
        g.sync.dma_start(T.kd[:], T.k[:]).then_inc(S.slk, 16)
        g.scalar.dma_start(T.vd[:], T.v[:]).then_inc(S.slv, 16)
        g.wait_ge(S.slk, 16)
        g.remote_dma(out_ap=T.gkv[:, slot * W:slot * W + KW], in_ap=T.kd[:], remote_sem=S["sgk%d" % slot],
                     local_sem=S.sx, pid=pid, routing_id=rid, dma_engine_mask=m)
        g.wait_ge(S.slv, 16)
        g.remote_dma(out_ap=T.gkv[:, slot * W + KW:(slot + 1) * W], in_ap=T.vd[:], remote_sem=S["sgv%d" % slot],
                     local_sem=S.sx, pid=pid, routing_id=rid, dma_engine_mask=m)
        g.wait_ge(S.sx, 2 * NSHIP)
        return

    if is_root:
        g.sync.dma_start(T.qd[:], T.q[:]).then_inc(S.sqd, 16)
        g.sync.wait_ge(S.sqd, 16)
        g.scalar.wait_ge(S.sqd, 16)
        g.scalar.dma_start(T.qs[:], T.q[:]).then_inc(S.sq, 16)
    else:
        g.sync.dma_start(T.hd[0:64, :], T.k[:, hb + keep:hb + BW]).then_inc(S.slh, 16)
        g.scalar.dma_start(T.hd[64:128, :], T.v[keep:BW, hb:hb + BW]).then_inc(S.slh, 16)
    g.sync.dma_start(T.kv[:, 0:KW], T.k[:]).then_inc(S.slk, 16)
    g.scalar.dma_start(T.kv[:, KW:W], T.v[:]).then_inc(S.slv, 16)

    if is_root:
        m = topo.mask(core, cores[sites[0]])
        ids = []
        for s in sites[::-1]:
            m &= topo.mask(core, cores[s])
            rid, pid = topo.addr(cores[s], core)
            ids.append(DstId(rid=rid, pnc=pid))
        g.wait_ge(S.sqd, 16)
        g.remote_dma_fused([RemoteDMATransfer(dst_ids=ids, dma_engine_mask=_engines(m, NQ), remote_sem=S.sq,
                                              srcs=[T.qd[:]], dsts=[T.qs[:] for s in sites], alu_op=0)],
                           local_sem=S.sx)
        for i in range(len(sites)):
            g.sync.wait_ge(S["sh%d" % i], NH)
            g.sync.dma_start(T.hk[:, i * HP:(i + 1) * HP], T.hl[i, 0:64, :]).then_inc(S.shk, 16)
            g.scalar.wait_ge(S["sh%d" % i], NH)
            g.scalar.dma_start(T.hv[i * HP:(i + 1) * HP, :], T.hl[i, 64:128, :]).then_inc(S.shv, 16)
    else:
        j = sites.index(rank)
        d = cores[root]
        rrid, rpid = topo.addr(d, core)
        rmask = topo.mask(core, d)
        g.wait_ge(S.slh, 32)
        g.remote_dma(out_ap=T.hl[j], in_ap=T.hd[:], remote_sem=S["sh%d" % j],
                     local_sem=S.sx, pid=rpid, routing_id=rrid, dma_engine_mask=_engines(rmask, NH))

    own_k, own_v = [(S.slk, 16)], [(S.slv, 16)]
    if is_root:
        groups = [(T.kv, 0, T.kv, KW, KB, BW, own_k, own_v)]
    else:
        groups = [(T.kv, 0, T.kv, KW, KB - 1, BW, own_k, own_v), (T.kv, hb, T.kv, KW + hb, 1, keep, [], [])]
    for i in range(len(guests[rank])):
        groups.append((T.gkv, i * W, T.gkv, i * W + KW, KB, BW,
                       [(S["sgk%d" % i], NSHIP)], [(S["sgv%d" % i], NSHIP)]))
    if is_root:
        groups.append((T.hk, 0, T.hv, 0, 1, HP * len(sites), [(S.shk, 16 * len(sites))], [(S.shv, 16 * len(sites))]))
    ngroups = len(groups)
    nblocks = sum(gr[4] for gr in groups)

    g.vector.memset(T.zero[:], 0.0).then_inc(S.sz, 1)
    g.vector.wait_ge(S.sz, 1)

    def scores(i):
        kbuf, kc, vbuf, vc, nb, npos, kw, vw = groups[i]
        for sem, val in kw:
            g.tensor.wait_ge(sem, val)
        ps = T["ps%d" % i]
        for b in range(nb):
            g.tensor.matmul(ps[0:npos, b * QP:(b + 1) * QP], kbuf[:, kc + b * BW:kc + b * BW + npos], T.qs[:],
                            start=True, stop=True).then_inc(S["sm%d" % i], 1)
        g.vector.wait_ge(S["sm%d" % i], nb)
        g.vector.tensor_tensor(T.sb[0:npos, i * SW:i * SW + nb * QP], ps[0:npos, 0:nb * QP],
                               T.zero[0:npos, 0:nb * QP], AluOpType.max).then_inc(S["sr%d" % i], 1)

    def values(i):
        kbuf, kc, vbuf, vc, nb, npos, kw, vw = groups[i]
        for sem, val in vw:
            g.tensor.wait_ge(sem, val)
        g.tensor.wait_ge(S["sr%d" % i], 1)
        for b in range(nb):
            g.tensor.matmul(T.po[:, 0:QP], vbuf[0:npos, vc + b * BW:vc + (b + 1) * BW],
                            T.sb[0:npos, i * SW + b * QP:i * SW + (b + 1) * QP],
                            start=(i == 0 and b == 0), stop=(i == ngroups - 1 and b == nb - 1)).then_inc(S.so, 1)

    g.tensor.wait_ge(S.sq, 16 if is_root else NQ)
    for i in range(ngroups):
        scores(i)
        if i > 0:
            values(i - 1)
    values(ngroups - 1)
    g.vector.wait_ge(S.so, nblocks)

    if not is_root:
        g.vector.tensor_copy(T.ob[:], T.po[:, 0:QP]).then_inc(S.sc, 1)
        g.wait_ge(S.sc, 1)
        g.remote_dma(out_ap=T.land[:, j * QP:(j + 1) * QP], in_ap=T.ob[:], remote_sem=S["sa%d" % j],
                     local_sem=S.sx, pid=rpid, routing_id=rrid, dma_engine_mask=_engines(rmask, NO))
        g.wait_ge(S.sx, NH + NO)
        return

    prev = T.po[:, 0:QP]
    for j in range(len(sites)):
        last = j == len(sites) - 1
        g.vector.wait_ge(S["sa%d" % j], NO)
        if j > 0:
            g.vector.wait_ge(S.sv, j)
        out = T.ob[:] if last else T.acc[:, j * QP:(j + 1) * QP]
        g.vector.tensor_tensor(out, prev, T.land[:, j * QP:(j + 1) * QP],
                               AluOpType.add).then_inc(S.sc if last else S.sv, 1)
        prev = out
    g.sync.wait_ge(S.sc, 1)
    g.sync.dma_start(T.y[:], T.ob[:]).then_inc(S.sy, 16)
    g.sync.wait_ge(S.sy, 16)
    g.wait_ge(S.sx, NQ)
